import numpy as np, ml_dtypes
CORES = [17,57,65,89,97,121]
N = 6
import mx_ref
NC = 128
BF = ml_dtypes.bfloat16
def cut(t, i, w=512):
    return t[:, w * i:w * i + w]
def tile(rs):
    return np.stack(rs, axis=2).reshape(128, -1).astype(BF)
def onehot(t, r):
    own, p, b = t[:, :NC], t[:, NC:2 * NC], t[:, 2 * NC:]
    return tile([((own == r) & (p == np.arange(128)[:, None]) & (b == f)).astype(np.float32) for f in range(4)])
def setup_inputs(rng):
    def f(*shape):
        return mx_ref.flush((rng.standard_normal(shape, dtype=np.float32) * np.exp2(rng.integers(-2, 3, shape[:-1] + (1,)))).astype(BF))
    t = np.concatenate([rng.integers(0, N, (N, 1, NC)), rng.integers(0, 128, (N, 1, NC)), rng.integers(0, 4, (N, 1, NC))], axis=2)
    return {"tg": np.broadcast_to(t, (N, 128, 3 * NC)).astype(BF).copy(), "tab": f(N, 128, 4 * 512), "w": f(N, 128, 512)}
def setup_inputs_blocks(rng):
    d = setup_inputs(rng)
    for k in ("tab", "w"): d[k] = mx_ref.spread(d[k], rng, 4)
    return d
def setup_inputs_wide(rng):
    d = setup_inputs(rng)
    for k in ("tab", "w"): d[k] = mx_ref.flush((d[k].astype(np.float32) * np.exp2(rng.integers(-6, 7, (N, 1, 1))).astype(np.float32)).astype(BF))
    return d
def setup_inputs_hot(rng):
    d = setup_inputs(rng); t = d["tg"].astype(np.float32); t[:, :, :NC] = rng.integers(0, N); t[:, :, NC:2 * NC] = np.broadcast_to(rng.integers(0, 4, (N, 1, NC)), (N, 128, NC))
    d["tg"] = t.astype(BF)
    return d
def reference(tg, tab, w):
    y = np.zeros((N, 128, NC), np.float32)
    for j in range(N):
        qw = mx_ref.quantize(w[j])
        for r in range(N):
            o = mx_ref.quantize(onehot(tg[j].astype(np.float32), r))
            e = mx_ref.quantize(tile([mx_ref.matmul(mx_ref.quantize(cut(tab[r], f)), o) for f in range(4)]))
            p = mx_ref.matmul(qw, e)
            y[j] = p if r == 0 else y[j] + p
    return {"y": y}

@@ -1,0 +1,288 @@
+import math
+from concourse.bass import DstId, RemoteDMATransfer
+from concourse.mybir import dt, AluOpType, ActivationFunctionType
+
+NC = 128
+EPS = 2.0 ** -20
+BMUL = (-1.0, EPS, 1.0, 2.0)
+LN4 = math.log(4.0)
+
+SCRATCH = {
+    "rcol": ("sbuf", [128, 8], "float32"),
+    "pi": ("sbuf", [128, 8], "float32"),
+    "ec": ("sbuf", [128, 8], "float32"),
+    "kc": ("sbuf", [128, 8], "bfloat16"),
+    "tgb": ("sbuf", [128, 384], "bfloat16"),
+    "tt": ("sbuf", [128, 384], "bfloat16"),
+    "pv": ("sbuf", [128, 4], "float32"),
+    "bm": ("sbuf", [128, 4], "float32"),
+    "pb": ("sbuf", [128, 4], "float32"),
+    "eo": ("sbuf", [128, 8], "bfloat16"),
+    "keyl": ("sbuf", [128, 8], "bfloat16"),
+    "la": ("sbuf", [128, 8], "bfloat16"),
+    "lb": ("sbuf", [128, 8], "bfloat16"),
+    "wk": ("sbuf", [128, 768], "bfloat16"),
+    "mk": ("sbuf", [128, 384], "bfloat16"),
+    "xs": ("sbuf", [128, 768], "bfloat16"),
+    "xt": ("sbuf", [128, 768], "bfloat16"),
+    "o": ("sbuf", [128, 3072], "bfloat16"),
+    "qo": ("sbuf", [128, 768], "float8_e4m3fn_x4"),
+    "so": ("sbuf", [128, 768], "uint8"),
+    "e": ("sbuf", [128, 3072], "bfloat16"),
+    "qe": ("sbuf", [128, 768], "float8_e4m3fn_x4"),
+    "se": ("sbuf", [128, 768], "uint8"),
+    "tabb": ("sbuf", [128, 2048], "bfloat16"),
+    "qt": ("sbuf", [128, 512], "float8_e4m3fn_x4"),
+    "st": ("sbuf", [128, 512], "uint8"),
+    "wb": ("sbuf", [128, 512], "bfloat16"),
+    "qw": ("sbuf", [128, 128], "float8_e4m3fn_x4"),
+    "sw": ("sbuf", [128, 128], "uint8"),
+    "le": ("sbuf", [128, 640], "float8_e4m3fn_x4"),
+    "ls": ("sbuf", [128, 640], "uint8"),
+    "rk": ("sbuf", [128, 8], "bfloat16"),
+    "rc": ("sbuf", [128, 128], "float8_e4m3fn_x4"),
+    "rs": ("sbuf", [128, 128], "uint8"),
+    "yb": ("sbuf", [128, 128], "float32"),
+    "z": ("psum", [128, 4096], "float32"),
+}
+GROUPS = ("S", "A", "B0", "B1", "B2")
+SEMAPHORES = (
+    ["ldtg", "ldt0", "ldt1", "ldw", "sty", "rc", "pi", "ec", "kc", "tgz", "wz", "mz", "tt", "pvbm", "pb", "eo", "key",
+     "qt", "qw", "yz", "yc", "loc", "ida", "idb", "ea0", "ea1", "eb0", "eb1", "eb2", "rid", "rcod", "rsca", "rloc"]
+    + ["%s%s" % (n, x) for n in ("ex", "sc", "xt") for x in ("S", "A", "B")]
+    + ["%s%s" % (n, x) for n in ("oh", "qo", "ce", "qe") for x in GROUPS]
+    + ["z%s%d" % (x, f) for x in GROUPS for f in range(4)]
+)
+
+
+def bits(mask):
+    return [1 << i for i in range(mask.bit_length()) if mask >> i & 1]
+
+
+def split(mask, n):
+    b = bits(mask)
+    k = len(b) // n
+    return [sum(b[i * k:(i + 1) * k]) for i in range(n)]
+
+
+def make_plan(T, topo):
+    C = list(T.cores)
+    R = range(len(C))
+    direct = {r: [j for j in R if j != r and topo.may_write(C[r], C[j])] for r in R}
+    cross = {r: [j for j in R if j != r and not topo.may_write(C[r], C[j])] for r in R}
+    lane, relay, order = {}, {}, {}
+    for r in R:
+        cand = [c for c in range(topo.CHIPS * topo.CORES_PER_CHIP)
+                if topo.chip(c) == topo.chip(C[r]) and c not in C and all(topo.may_write(c, C[j]) for j in cross[r])]
+        cand.sort(key=lambda c: (topo.die(c) != topo.die(C[r]), c))
+        for d, j in enumerate(cross[r]):
+            lane[r, j] = (cross[j].index(r) + d) % len(cross[r])
+            relay[r, j] = cand[lane[r, j]]
+        order[r] = sorted(cross[r], key=lambda j: (lane[r, j] + 1) % len(cross[r]))
+    return C, direct, cross, relay, order
+
+
+def run_relay(g, core, T, topo, C, relay, order, r, j):
+    sem = T.sem
+    rid, pid = topo.addr(C[j])[:2]
+    off = topo.mask(core, C[j])
+    k = len(bits(off))
+    n_on = len(bits(topo.mask(C[r], core)))
+    n_in = n_on // 2 if order[r].index(j) < 2 else n_on
+    n_id = len(bits(topo.mask(C[r], core) & ~off))
+    ib = order[j].index(r)
+    slot = 2 + ib
+    g.wait_ge(sem["rid"], n_id)
+    g.remote_dma(T.lb[:, 2 * ib:2 * ib + 2], T.rk[:, 0:2], sem["idb"], sem["rloc"], pid, rid, off)
+    g.wait_ge(sem["rcod"], n_in)
+    g.remote_dma(T.le[:, NC * slot:NC * slot + NC].bitcast(dt.uint8), T.rc[:, 0:NC].bitcast(dt.uint8),
+                 sem["eb%d" % ib], sem["rloc"], pid, rid, off)
+    g.wait_ge(sem["rsca"], n_in)
+    g.remote_dma(T.ls[:, NC * slot:NC * slot + NC], T.rs[:, 0:NC], sem["eb%d" % ib], sem["rloc"], pid, rid, off)
+    g.wait_ge(sem["rloc"], 3 * k)
+
+
+def rank_program(g, core, T, topo):
+    C, direct, cross, relay, order = make_plan(T, topo)
+    rank = T.rank_of(core)
+    if rank is None:
+        for (r, j), c in relay.items():
+            if c == core:
+                run_relay(g, core, T, topo, C, relay, order, r, j)
+        return
+    sem = T.sem
+    v, s, t, sy = g.vector, g.scalar, g.tensor, g.sync
+    ADD, SUB, MUL, EQ = AluOpType.add, AluOpType.subtract, AluOpType.mult, AluOpType.is_equal
+    EXP, COPY = ActivationFunctionType.Exp, ActivationFunctionType.Copy
+    mine, near = order[rank], direct[rank]
+    COL = {"S": (0, 128), "A": (128, 256), "B0": (384, 128), "B1": (512, 128), "B2": (640, 128), "B": (384, 384)}
+    BANK = {"S": 0, "A": 4, "B0": 0, "B1": 4, "B2": 0}
+
+    for a in (0, 1): sy.dma_start(T.tgb[32 * a + 31:32 * a + 32, :], T.tg[a:a + 1, :]).then_inc(sem["ldtg"], 16)
+    for a in (2, 3): s.dma_start(T.tgb[32 * a + 31:32 * a + 32, :], T.tg[a:a + 1, :]).then_inc(sem["ldtg"], 16)
+    sy.dma_start(T.tabb[:, 0:1024], T.tab[:, 0:1024]).then_inc(sem["ldt0"], 16)
+    sy.dma_start(T.tabb[:, 1024:2048], T.tab[:, 1024:2048]).then_inc(sem["ldt1"], 16)
+    sy.dma_start(T.wb[:], T.w[:]).then_inc(sem["ldw"], 16)
+    sy.wait_ge(sem["yc"], 1)
+    sy.dma_start(T.y[:], T.yb[:]).then_inc(sem["sty"], 16)
+    sy.wait_ge(sem["sty"], 16)
+
+    def copy_e(q, x, f):
+        c0, n = COL[x]
+        b0 = 512 * (BANK[x] + f)
+        q.wait_ge(sem["z%s%d" % (x, f)], 1)
+        out = T.e[:, 4 * c0 + f:4 * (c0 + n):4]
+        if q is s:
+            s.activation(out, T.z[:, b0:b0 + n], COPY).then_inc(sem["ce" + x], 1)
+        else:
+            v.tensor_copy(out, T.z[:, b0:b0 + n]).then_inc(sem["ce" + x], 1)
+
+    s.wait_ge(sem["rc"], 1)
+    s.activation(T.ec[:, 0:1], T.rcol[:, 0:1], EXP, scale=LN4).then_inc(sem["ec"], 1)
+    s.wait_ge(sem["tt"], 1)
+    s.activation(T.eo[:, 0:4], T.tt[:, 31:128:32], EXP, scale=LN4).then_inc(sem["eo"], 1)
+    for f in range(4): copy_e(s, "S", f)
+    for f in (0, 2): copy_e(s, "A", f)
+    for f in range(4): copy_e(s, "B0", f)
+    for f in range(4): copy_e(s, "B1", f)
+    for f in (0, 2): copy_e(s, "B2", f)
+
+    v.memset(T.rcol[:], float(rank)).then_inc(sem["rc"], 1)
+    for a in range(4):
+        v.memset(T.tgb[32 * a:32 * a + 31, :], 0.0).then_inc(sem["tgz"], 1)
+    v.memset(T.mk[:], 1.0).then_inc(sem["mz"], 1)
+    v.memset(T.wk[:], 0.0).then_inc(sem["wz"], 1)
+    v.wait_ge(sem["mz"], 1)
+    v.memset(T.mk[:, 0:384:32], 0.0).then_inc(sem["mz"], 1)
+    v.wait_ge(sem["pi"], 1)
+    v.wait_ge(sem["ec"], 1)
+    for b in range(4):
+        v.tensor_scalar(T.kc[:, b:b + 1], T.pi[:, 0:1], BMUL[b], T.ec[:, 0:1], MUL, MUL).then_inc(sem["kc"], 1)
+    v.wait_ge(sem["tgz"], 4)
+    v.wait_ge(sem["ldtg"], 64)
+    v.transpose(T.tt[:], T.tgb[:]).then_inc(sem["tt"], 1)
+    v.wait_ge(sem["tt"], 1)
+    v.tensor_scalar(T.pv[:], T.tt[:, 159:256:32], 128.0, None, ADD).then_inc(sem["pvbm"], 1)
+    v.tensor_scalar(T.bm[:], T.tt[:, 287:384:32], 1.0 - EPS, None, SUB).then_inc(sem["pvbm"], 1)
+    v.wait_ge(sem["pvbm"], 2)
+    v.tensor_tensor(T.pb[:], T.pv[:], T.bm[:], MUL).then_inc(sem["pb"], 1)
+    v.wait_ge(sem["pb"], 1)
+    v.wait_ge(sem["eo"], 1)
+    v.tensor_tensor(T.keyl[0:64, 0:2], T.pb[0:64, 0:4:2], T.eo[0:64, 0:4:2], MUL).then_inc(sem["key"], 1)
+    v.tensor_tensor(T.keyl[64:128, 0:2], T.pb[64:128, 1:4:2], T.eo[64:128, 1:4:2], MUL).then_inc(sem["key"], 1)
+    v.wait_ge(sem["wz"], 1)
+    v.tensor_tensor(T.wk[:, 0:128:32], T.pb[:], T.eo[:, 0:4], MUL).then_inc(sem["exS"], 1)
+
+    def expand(L, x):
+        c0, n = COL[x]
+        w2 = n // 64
+        for h in range(2):
+            for o in (0, 64):
+                v.tensor_copy(T.wk[o:o + 64, c0 + 32 * h:c0 + n:64], L[64 * h:64 * h + 64, 0:w2]).then_inc(sem["ex" + x], 1)
+
+    def spread(x, heads):
+        c0, n = COL[x]
+        v.wait_ge(sem["ex" + x], heads)
+        v.tensor_tensor_scan(T.xs[:, c0:c0 + n], T.mk[:, 0:n], T.wk[:, c0:c0 + n], 0.0, MUL, ADD).then_inc(sem["sc" + x], 1)
+        v.wait_ge(sem["sc" + x], 1)
+        v.transpose(T.xt[:, c0:c0 + n], T.xs[:, c0:c0 + n]).then_inc(sem["xt" + x], 1)
+        v.wait_ge(sem["xt" + x], 1)
+
+    def onehots(x):
+        c0, n = COL[x]
+        for b in range(4):
+            v.tensor_scalar(T.o[:, 4 * c0 + b:4 * (c0 + n):4], T.xt[:, c0:c0 + n], T.kc[:, b:b + 1], None, EQ).then_inc(sem["oh" + x], 1)
+        v.wait_ge(sem["oh" + x], 4)
+        v.quantize_mx(T.qo[:, c0:c0 + n], T.so[:, c0:c0 + n], T.o[:, 4 * c0:4 * (c0 + n)]).then_inc(sem["qo" + x], 1)
+
+    def quant_e(x):
+        c0, n = COL[x]
+        v.wait_ge(sem["ce" + x], 4)
+        v.quantize_mx(T.qe[:, c0:c0 + n], T.se[:, c0:c0 + n], T.e[:, 4 * c0:4 * (c0 + n)]).then_inc(sem["qe" + x], 1)
+
+    v.wait_ge(sem["mz"], 2)
+    v.wait_ge(sem["kc"], 4)
+    spread("S", 1)
+    onehots("S")
+    for i in range(2):
+        v.wait_ge(sem["ldt%d" % i], 16)
+        v.quantize_mx(T.qt[:, 256 * i:256 * i + 256], T.st[:, 256 * i:256 * i + 256], T.tabb[:, 1024 * i:1024 * i + 1024]).then_inc(sem["qt"], 1)
+    v.wait_ge(sem["ida"], len(near) * len(bits(topo.mask(core, C[near[0]]))))
+    expand(T.la, "A")
+    spread("A", 4)
+    onehots("A")
+    v.wait_ge(sem["ldw"], 16)
+    v.quantize_mx(T.qw[:], T.sw[:], T.wb[:]).then_inc(sem["qw"], 1)
+    quant_e("S")
+    for f in (1, 3): copy_e(v, "A", f)
+    quant_e("A")
+    v.wait_ge(sem["idb"], sum(len(bits(topo.mask(relay[j, rank], core))) for j in mine))
+    expand(T.lb, "B")
+    spread("B", 4)
+    for x in ("B0", "B1", "B2"): onehots(x)
+    quant_e("B0")
+    quant_e("B1")
+    for f in (1, 3): copy_e(v, "B2", f)
+    quant_e("B2")
+    v.wait_ge(sem["yz"], 1)
+    v.tensor_copy(T.yb[:], T.z[:, 2048:2048 + NC]).then_inc(sem["yc"], 1)
+
+    t.wait_ge(sem["qt"], 2)
+    free = {"S": None, "A": None, "B0": "S", "B1": "A", "B2": "B0"}
+    for x in GROUPS:
+        c0, n = COL[x]
+        t.wait_ge(sem["qo" + x], 1)
+        if free[x]:
+            t.wait_ge(sem["ce" + free[x]], 4)
+        for f in range(4):
+            b0 = 512 * (BANK[x] + f)
+            t.matmul_mx(T.z[:, b0:b0 + n], T.qt[:, 128 * f:128 * f + 128], T.st[:, 128 * f:128 * f + 128],
+                        T.qo[:, c0:c0 + n], T.so[:, c0:c0 + n], True, True).then_inc(sem["z%s%d" % (x, f)], 1)
+    yo = T.z[:, 2048:2048 + NC]
+    t.wait_ge(sem["ceB1"], 4)
+    t.wait_ge(sem["qw"], 1)
+    t.wait_ge(sem["qeS"], 1)
+    t.matmul_mx(yo, T.qw[:], T.sw[:], T.qe[:, 0:NC], T.se[:, 0:NC], True, False)
+    half = len(bits(topo.mask(core, C[near[0]]))) // len(near)
+    for i in range(len(near)):
+        t.wait_ge(sem["ea%d" % i], 2 * half)
+        t.matmul_mx(yo, T.qw[:], T.sw[:], T.le[:, NC * i:NC * i + NC], T.ls[:, NC * i:NC * i + NC], False, False)
+    arr = sorted(range(len(mine)), key=lambda i: order[mine[i]].index(rank))
+    for i in arr:
+        p = 2 + i
+        t.wait_ge(sem["eb%d" % i], 2 * len(bits(topo.mask(relay[mine[i], rank], core))))
+        m = t.matmul_mx(yo, T.qw[:], T.sw[:], T.le[:, NC * p:NC * p + NC], T.ls[:, NC * p:NC * p + NC], False, i == arr[-1])
+    m.then_inc(sem["yz"], 1)
+
+    g.iota(T.pi[:, 0:1], [[0, 1]], 128, 1, allow_small_or_imprecise_dtypes=True).then_inc(sem["pi"], 1)
+    rel = [relay[rank, j] for j in mine]
+    on = topo.mask(core, rel[0])
+    off = topo.mask(core, C[near[0]])
+    sent = [0]
+
+    def move(dsts, mask, rsem, src, outs):
+        return RemoteDMATransfer(dst_ids=[DstId(rid=topo.addr(d)[0], pnc=topo.addr(d)[1]) for d in dsts],
+                                 dma_engine_mask=mask, remote_sem=sem[rsem], srcs=[src], dsts=outs)
+
+    def send(transfers, masks):
+        g.remote_dma_fused(transfers, local_sem=sem["loc"])
+        sent[0] += sum(len(bits(m)) for m in masks)
+
+    g.wait_ge(sem["key"], 2)
+    send([move(rel, on & ~off, "rid", T.keyl[:, 0:2], [T.rk[:, 0:2]] * len(rel))], [on & ~off])
+    ai = [direct[j].index(rank) for j in near]
+    send([move([C[j] for j in near], off, "ida", T.keyl[:, 0:2], [T.la[:, 2 * a:2 * a + 2] for a in ai])], [off])
+    g.wait_ge(sem["qeA"], 1)
+    ms = split(off, len(near))
+    jobs = list(enumerate(zip(near, ai, ms)))
+    send([move([C[j]], m, "ea%d" % a, T.qe[:, 128 + NC * k:256 + NC * k].bitcast(dt.uint8),
+               [T.le[:, NC * a:NC * a + NC].bitcast(dt.uint8)]) for k, (j, a, m) in jobs], ms)
+    send([move([C[j]], m, "ea%d" % a, T.se[:, 128 + NC * k:256 + NC * k], [T.ls[:, NC * a:NC * a + NC]])
+          for k, (j, a, m) in jobs], ms)
+    for ks in ((0, 1), (2,)):
+        for k in ks: g.wait_ge(sem["qeB%d" % k], 1)
+        ms = split(on, len(ks))
+        send([move([rel[k]], m, "rcod", T.qe[:, 384 + NC * k:512 + NC * k].bitcast(dt.uint8),
+                   [T.rc[:, 0:NC].bitcast(dt.uint8)]) for k, m in zip(ks, ms)], ms)
+        send([move([rel[k]], m, "rsca", T.se[:, 384 + NC * k:512 + NC * k], [T.rs[:, 0:NC]]) for k, m in zip(ks, ms)], ms)
+    g.wait_ge(sem["loc"], sent[0])

@@ -22,7 +22,7 @@ SCRATCH = {
     "la": ("sbuf", [128, 8], "bfloat16"),
     "lb": ("sbuf", [128, 8], "bfloat16"),
     "wk": ("sbuf", [128, 768], "bfloat16"),
-    "mk": ("sbuf", [128, 384], "bfloat16"),
+    "mk": ("sbuf", [128, 256], "bfloat16"),
     "xs": ("sbuf", [128, 768], "bfloat16"),
     "xt": ("sbuf", [128, 768], "bfloat16"),
     "o": ("sbuf", [128, 3072], "bfloat16"),
@@ -41,16 +41,16 @@ SCRATCH = {
     "ls": ("sbuf", [128, 640], "uint8"),
     "rk": ("sbuf", [128, 8], "bfloat16"),
     "rc": ("sbuf", [128, 128], "float8_e4m3fn_x4"),
-    "rs": ("sbuf", [128, 128], "uint8"),
+    "rs": ("sbuf", [128, 256], "uint8"),
     "yb": ("sbuf", [128, 128], "float32"),
     "z": ("psum", [128, 4096], "float32"),
 }
 GROUPS = ("S", "A", "B0", "B1", "B2")
 SEMAPHORES = (
     ["ldtg", "ldt0", "ldt1", "ldw", "sty", "rc", "pi", "ec", "kc", "tgz", "wz", "mz", "tt", "pvbm", "pb", "eo", "key",
-     "qt", "qw", "yz", "yc", "loc", "ida", "idb", "ea0", "ea1", "eb0", "eb1", "eb2", "rid", "rcod", "rsca", "rloc"]
-    + ["%s%s" % (n, x) for n in ("ex", "sc", "xt") for x in ("S", "A", "B")]
-    + ["%s%s" % (n, x) for n in ("oh", "qo", "ce", "qe") for x in GROUPS]
+     "qt", "qw", "yz", "yc", "loc", "ida", "idb", "ea0", "ea1", "eb0", "eb1", "eb2", "rid", "rcod", "rsca", "rscb", "rloc",
+     "exS", "exA", "exB"]
+    + ["%s%s" % (n, x) for n in ("sc", "xt", "oh", "qo", "ce", "qe") for x in GROUPS]
     + ["z%s%d" % (x, f) for x in GROUPS for f in range(4)]
 )
 
@@ -82,24 +82,34 @@ def make_plan(T, topo):
     return C, direct, cross, relay, order
 
 
-def run_relay(g, core, T, topo, C, relay, order, r, j):
+def run_relay(g, core, T, topo, C, order, r, j):
     sem = T.sem
-    rid, pid = topo.addr(C[j])[:2]
     off = topo.mask(core, C[j])
-    k = len(bits(off))
     n_on = len(bits(topo.mask(C[r], core)))
-    n_in = n_on // 2 if order[r].index(j) < 2 else n_on
     n_id = len(bits(topo.mask(C[r], core) & ~off))
-    ib = order[j].index(r)
-    slot = 2 + ib
+    k = order[r].index(j)
+    sent = [0]
+
+    def scales(to, col):
+        rid, pid = topo.addr(C[to])[:2]
+        i = order[to].index(r)
+        g.remote_dma(T.ls[:, NC * (2 + i):NC * (3 + i)], T.rs[:, col:col + NC], sem["eb%d" % i], sem["rloc"], pid, rid, off)
+        sent[0] += len(bits(off))
+
+    rid, pid = topo.addr(C[j])[:2]
+    i = order[j].index(r)
     g.wait_ge(sem["rid"], n_id)
-    g.remote_dma(T.lb[:, 2 * ib:2 * ib + 2], T.rk[:, 0:2], sem["idb"], sem["rloc"], pid, rid, off)
-    g.wait_ge(sem["rcod"], n_in)
-    g.remote_dma(T.le[:, NC * slot:NC * slot + NC].bitcast(dt.uint8), T.rc[:, 0:NC].bitcast(dt.uint8),
-                 sem["eb%d" % ib], sem["rloc"], pid, rid, off)
-    g.wait_ge(sem["rsca"], n_in)
-    g.remote_dma(T.ls[:, NC * slot:NC * slot + NC], T.rs[:, 0:NC], sem["eb%d" % ib], sem["rloc"], pid, rid, off)
-    g.wait_ge(sem["rloc"], 3 * k)
+    g.remote_dma(T.lb[:, 2 * i:2 * i + 2], T.rk[:, 0:2], sem["idb"], sem["rloc"], pid, rid, off)
+    if k < 2:
+        g.wait_ge(sem["rsca"], n_on)
+        scales(j, 0)
+    g.wait_ge(sem["rcod"], n_on)
+    g.remote_dma(T.le[:, NC * (2 + i):NC * (3 + i)].bitcast(dt.uint8), T.rc[:, 0:NC].bitcast(dt.uint8),
+                 sem["eb%d" % i], sem["rloc"], pid, rid, off)
+    if k == 0:
+        g.wait_ge(sem["rscb"], n_on)
+        scales(order[r][2], NC)
+    g.wait_ge(sem["rloc"], sent[0] + 2 * len(bits(off)))
 
 
 def rank_program(g, core, T, topo):
@@ -108,7 +118,7 @@ def rank_program(g, core, T, topo):
     if rank is None:
         for (r, j), c in relay.items():
             if c == core:
-                run_relay(g, core, T, topo, C, relay, order, r, j)
+                run_relay(g, core, T, topo, C, order, r, j)
         return
     sem = T.sem
     v, s, t, sy = g.vector, g.scalar, g.tensor, g.sync
@@ -153,11 +163,7 @@ def rank_program(g, core, T, topo):
     v.memset(T.mk[:], 1.0).then_inc(sem["mz"], 1)
     v.memset(T.wk[:], 0.0).then_inc(sem["wz"], 1)
     v.wait_ge(sem["mz"], 1)
-    v.memset(T.mk[:, 0:384:32], 0.0).then_inc(sem["mz"], 1)
-    v.wait_ge(sem["pi"], 1)
-    v.wait_ge(sem["ec"], 1)
-    for b in range(4):
-        v.tensor_scalar(T.kc[:, b:b + 1], T.pi[:, 0:1], BMUL[b], T.ec[:, 0:1], MUL, MUL).then_inc(sem["kc"], 1)
+    v.memset(T.mk[:, 0:256:32], 0.0).then_inc(sem["mz"], 1)
     v.wait_ge(sem["tgz"], 4)
     v.wait_ge(sem["ldtg"], 64)
     v.transpose(T.tt[:], T.tgb[:]).then_inc(sem["tt"], 1)
@@ -172,6 +178,10 @@ def rank_program(g, core, T, topo):
     v.tensor_tensor(T.keyl[64:128, 0:2], T.pb[64:128, 1:4:2], T.eo[64:128, 1:4:2], MUL).then_inc(sem["key"], 1)
     v.wait_ge(sem["wz"], 1)
     v.tensor_tensor(T.wk[:, 0:128:32], T.pb[:], T.eo[:, 0:4], MUL).then_inc(sem["exS"], 1)
+    v.wait_ge(sem["pi"], 1)
+    v.wait_ge(sem["ec"], 1)
+    for b in range(4):
+        v.tensor_scalar(T.kc[:, b:b + 1], T.pi[:, 0:1], BMUL[b], T.ec[:, 0:1], MUL, MUL).then_inc(sem["kc"], 1)
 
     def expand(L, x):
         c0, n = COL[x]
@@ -179,19 +189,25 @@ def rank_program(g, core, T, topo):
         for h in range(2):
             for o in (0, 64):
                 v.tensor_copy(T.wk[o:o + 64, c0 + 32 * h:c0 + n:64], L[64 * h:64 * h + 64, 0:w2]).then_inc(sem["ex" + x], 1)
+        v.wait_ge(sem["ex" + x], 4)
 
-    def spread(x, heads):
+    def scan(x):
         c0, n = COL[x]
-        v.wait_ge(sem["ex" + x], heads)
         v.tensor_tensor_scan(T.xs[:, c0:c0 + n], T.mk[:, 0:n], T.wk[:, c0:c0 + n], 0.0, MUL, ADD).then_inc(sem["sc" + x], 1)
+
+    def turn(x):
+        c0, n = COL[x]
         v.wait_ge(sem["sc" + x], 1)
         v.transpose(T.xt[:, c0:c0 + n], T.xs[:, c0:c0 + n]).then_inc(sem["xt" + x], 1)
-        v.wait_ge(sem["xt" + x], 1)
 
-    def onehots(x):
+    def compare(x):
         c0, n = COL[x]
+        v.wait_ge(sem["xt" + x], 1)
         for b in range(4):
             v.tensor_scalar(T.o[:, 4 * c0 + b:4 * (c0 + n):4], T.xt[:, c0:c0 + n], T.kc[:, b:b + 1], None, EQ).then_inc(sem["oh" + x], 1)
+
+    def quant_o(x):
+        c0, n = COL[x]
         v.wait_ge(sem["oh" + x], 4)
         v.quantize_mx(T.qo[:, c0:c0 + n], T.so[:, c0:c0 + n], T.o[:, 4 * c0:4 * (c0 + n)]).then_inc(sem["qo" + x], 1)
 
@@ -201,16 +217,16 @@ def rank_program(g, core, T, topo):
         v.quantize_mx(T.qe[:, c0:c0 + n], T.se[:, c0:c0 + n], T.e[:, 4 * c0:4 * (c0 + n)]).then_inc(sem["qe" + x], 1)
 
     v.wait_ge(sem["mz"], 2)
+    v.wait_ge(sem["exS"], 1)
+    scan("S"); turn("S")
     v.wait_ge(sem["kc"], 4)
-    spread("S", 1)
-    onehots("S")
+    compare("S"); quant_o("S")
     for i in range(2):
         v.wait_ge(sem["ldt%d" % i], 16)
         v.quantize_mx(T.qt[:, 256 * i:256 * i + 256], T.st[:, 256 * i:256 * i + 256], T.tabb[:, 1024 * i:1024 * i + 1024]).then_inc(sem["qt"], 1)
     v.wait_ge(sem["ida"], len(near) * len(bits(topo.mask(core, C[near[0]]))))
     expand(T.la, "A")
-    spread("A", 4)
-    onehots("A")
+    scan("A"); turn("A"); compare("A"); quant_o("A")
     v.wait_ge(sem["ldw"], 16)
     v.quantize_mx(T.qw[:], T.sw[:], T.wb[:]).then_inc(sem["qw"], 1)
     quant_e("S")
@@ -218,8 +234,10 @@ def rank_program(g, core, T, topo):
     quant_e("A")
     v.wait_ge(sem["idb"], sum(len(bits(topo.mask(relay[j, rank], core))) for j in mine))
     expand(T.lb, "B")
-    spread("B", 4)
-    for x in ("B0", "B1", "B2"): onehots(x)
+    scan("B0"); scan("B1"); turn("B0"); scan("B2"); turn("B1")
+    compare("B0"); turn("B2"); quant_o("B0")
+    compare("B1"); quant_o("B1")
+    compare("B2"); quant_o("B2")
     quant_e("B0")
     quant_e("B1")
     for f in (1, 3): copy_e(v, "B2", f)
@@ -279,10 +297,18 @@ def rank_program(g, core, T, topo):
                [T.le[:, NC * a:NC * a + NC].bitcast(dt.uint8)]) for k, (j, a, m) in jobs], ms)
     send([move([C[j]], m, "ea%d" % a, T.se[:, 128 + NC * k:256 + NC * k], [T.ls[:, NC * a:NC * a + NC]])
           for k, (j, a, m) in jobs], ms)
-    for ks in ((0, 1), (2,)):
-        for k in ks: g.wait_ge(sem["qeB%d" % k], 1)
-        ms = split(on, len(ks))
-        send([move([rel[k]], m, "rcod", T.qe[:, 384 + NC * k:512 + NC * k].bitcast(dt.uint8),
-                   [T.rc[:, 0:NC].bitcast(dt.uint8)]) for k, m in zip(ks, ms)], ms)
-        send([move([rel[k]], m, "rsca", T.se[:, 384 + NC * k:512 + NC * k], [T.rs[:, 0:NC]]) for k, m in zip(ks, ms)], ms)
+
+    def codes(k):
+        send([move([rel[k]], on, "rcod", T.qe[:, 384 + NC * k:512 + NC * k].bitcast(dt.uint8), [T.rc[:, 0:NC].bitcast(dt.uint8)])], [on])
+
+    def scales(k, by, rsem, col):
+        send([move([rel[by]], on, rsem, T.se[:, 384 + NC * k:512 + NC * k], [T.rs[:, col:col + NC]])], [on])
+
+    for k in (0, 1):
+        g.wait_ge(sem["qeB%d" % k], 1)
+        scales(k, k, "rsca", 0)
+        codes(k)
+    g.wait_ge(sem["qeB2"], 1)
+    codes(2)
+    scales(2, 0, "rscb", NC)
     g.wait_ge(sem["loc"], sent[0])

@@ -1,28 +1,20 @@
-import math
 from concourse.bass import DstId, RemoteDMATransfer
 from concourse.mybir import dt, AluOpType, ActivationFunctionType
 
 NC = 128
-EPS = 2.0 ** -20
-BMUL = (-1.0, EPS, 1.0, 2.0)
-LN4 = math.log(4.0)
 
 SCRATCH = {
-    "rcol": ("sbuf", [128, 8], "float32"),
-    "pi": ("sbuf", [128, 8], "float32"),
-    "ec": ("sbuf", [128, 8], "float32"),
+    "r6": ("sbuf", [64, 8], "float32"),
     "kc": ("sbuf", [128, 8], "bfloat16"),
-    "tgb": ("sbuf", [128, 384], "bfloat16"),
-    "tt": ("sbuf", [128, 384], "bfloat16"),
-    "pv": ("sbuf", [128, 4], "float32"),
-    "bm": ("sbuf", [128, 4], "float32"),
-    "pb": ("sbuf", [128, 4], "float32"),
-    "eo": ("sbuf", [128, 8], "bfloat16"),
-    "keyl": ("sbuf", [128, 8], "bfloat16"),
+    "tgb": ("sbuf", [64, 128], "bfloat16"),
+    "tt": ("sbuf", [64, 128], "bfloat16"),
+    "ow": ("sbuf", [64, 4], "float32"),
+    "pb": ("sbuf", [64, 4], "float32"),
+    "kk": ("sbuf", [128, 16], "bfloat16"),
     "la": ("sbuf", [128, 8], "bfloat16"),
     "lb": ("sbuf", [128, 8], "bfloat16"),
     "wk": ("sbuf", [128, 768], "bfloat16"),
-    "mk": ("sbuf", [128, 256], "bfloat16"),
+    "mk": ("sbuf", [128, 128], "bfloat16"),
     "xs": ("sbuf", [128, 768], "bfloat16"),
     "xt": ("sbuf", [128, 768], "bfloat16"),
     "o": ("sbuf", [128, 3072], "bfloat16"),
@@ -45,9 +37,9 @@ SCRATCH = {
     "yb": ("sbuf", [128, 128], "float32"),
     "z": ("psum", [128, 4096], "float32"),
 }
-GROUPS = ("S", "A", "B0", "B1", "B2")
+GROUPS = ("S", "A0", "A1", "B0", "B1", "B2")
 SEMAPHORES = (
-    ["ldtg", "ldt0", "ldt1", "ldw", "sty", "rc", "pi", "ec", "kc", "tgz", "wz", "mz", "tt", "pvbm", "pb", "eo", "key",
+    ["ldtg", "ldt0", "ldt1", "ldw", "sty", "r6", "kc", "tgz", "wz", "mz", "tt", "ow", "pb0", "pb1", "pb2", "pb3", "key",
      "qt", "qw", "yz", "yc", "loc", "ida", "idb", "ea0", "ea1", "eb0", "eb1", "eb2", "rid", "rcod", "rsca", "rscb", "rloc",
      "exS", "exA", "exB"]
     + ["%s%s" % (n, x) for n in ("sc", "xt", "oh", "qo", "ce", "qe") for x in GROUPS]
@@ -63,6 +55,10 @@ def split(mask, n):
     b = bits(mask)
     k = len(b) // n
     return [sum(b[i * k:(i + 1) * k]) for i in range(n)]
+
+
+def id_masks(on, off, n):
+    return sorted(split(on, 4), key=lambda m: m & off)[:n]
 
 
 def make_plan(T, topo):
@@ -85,8 +81,9 @@ def make_plan(T, topo):
 def run_relay(g, core, T, topo, C, order, r, j):
     sem = T.sem
     off = topo.mask(core, C[j])
-    n_on = len(bits(topo.mask(C[r], core)))
-    n_id = len(bits(topo.mask(C[r], core) & ~off))
+    on = topo.mask(C[r], core)
+    n_on = len(bits(on))
+    n_id = len(bits(id_masks(on, off, len(order[r]))[0]))
     k = order[r].index(j)
     sent = [0]
 
@@ -123,13 +120,20 @@ def rank_program(g, core, T, topo):
     sem = T.sem
     v, s, t, sy = g.vector, g.scalar, g.tensor, g.sync
     ADD, SUB, MUL, EQ = AluOpType.add, AluOpType.subtract, AluOpType.mult, AluOpType.is_equal
-    EXP, COPY = ActivationFunctionType.Exp, ActivationFunctionType.Copy
+    COPY = ActivationFunctionType.Copy
     mine, near = order[rank], direct[rank]
-    COL = {"S": (0, 128), "A": (128, 256), "B0": (384, 128), "B1": (512, 128), "B2": (640, 128), "B": (384, 384)}
-    BANK = {"S": 0, "A": 4, "B0": 0, "B1": 4, "B2": 0}
+    COL = {x: (NC * i, NC) for i, x in enumerate(GROUPS)}
+    COL["A"], COL["B"] = (NC, 2 * NC), (3 * NC, 3 * NC)
+    BANK = {x: 4 * (i % 2) for i, x in enumerate(GROUPS)}
+    rel = [relay[rank, j] for j in mine]
+    on = topo.mask(core, rel[0])
+    off = topo.mask(core, C[near[0]])
+    idm = id_masks(on, off, len(rel))
+    half = split(off, len(near))
+    n_relay = len(bits(topo.mask(rel[0], C[mine[0]])))
 
-    for a in (0, 1): sy.dma_start(T.tgb[32 * a + 31:32 * a + 32, :], T.tg[a:a + 1, :]).then_inc(sem["ldtg"], 16)
-    for a in (2, 3): s.dma_start(T.tgb[32 * a + 31:32 * a + 32, :], T.tg[a:a + 1, :]).then_inc(sem["ldtg"], 16)
+    sy.dma_start(T.tgb[29:32, :], T.tg[0:1, :]).then_inc(sem["ldtg"], 16)
+    s.dma_start(T.tgb[61:64, :], T.tg[1:2, :]).then_inc(sem["ldtg"], 16)
     sy.dma_start(T.tabb[:, 0:1024], T.tab[:, 0:1024]).then_inc(sem["ldt0"], 16)
     sy.dma_start(T.tabb[:, 1024:2048], T.tab[:, 1024:2048]).then_inc(sem["ldt1"], 16)
     sy.dma_start(T.wb[:], T.w[:]).then_inc(sem["ldw"], 16)
@@ -137,63 +141,56 @@ def rank_program(g, core, T, topo):
     sy.dma_start(T.y[:], T.yb[:]).then_inc(sem["sty"], 16)
     sy.wait_ge(sem["sty"], 16)
 
-    def copy_e(q, x, f):
+    def copy_e(q, x, fs):
         c0, n = COL[x]
-        b0 = 512 * (BANK[x] + f)
-        q.wait_ge(sem["z%s%d" % (x, f)], 1)
-        out = T.e[:, 4 * c0 + f:4 * (c0 + n):4]
-        if q is s:
-            s.activation(out, T.z[:, b0:b0 + n], COPY).then_inc(sem["ce" + x], 1)
-        else:
-            v.tensor_copy(out, T.z[:, b0:b0 + n]).then_inc(sem["ce" + x], 1)
+        for f in fs:
+            b0 = 512 * (BANK[x] + f)
+            q.wait_ge(sem["z%s%d" % (x, f)], 1)
+            out = T.e[:, 4 * c0 + f:4 * (c0 + n):4]
+            if q is s:
+                s.activation(out, T.z[:, b0:b0 + n], COPY).then_inc(sem["ce" + x], 1)
+            else:
+                v.tensor_copy(out, T.z[:, b0:b0 + n]).then_inc(sem["ce" + x], 1)
 
-    s.wait_ge(sem["rc"], 1)
-    s.activation(T.ec[:, 0:1], T.rcol[:, 0:1], EXP, scale=LN4).then_inc(sem["ec"], 1)
-    s.wait_ge(sem["tt"], 1)
-    s.activation(T.eo[:, 0:4], T.tt[:, 31:128:32], EXP, scale=LN4).then_inc(sem["eo"], 1)
-    for f in range(4): copy_e(s, "S", f)
-    for f in (0, 2): copy_e(s, "A", f)
-    for f in range(4): copy_e(s, "B0", f)
-    for f in range(4): copy_e(s, "B1", f)
-    for f in (0, 2): copy_e(s, "B2", f)
+    def expand(q, L, l0, x):
+        c0, n = COL[x]
+        for h in (0, 1):
+            for o in (0, 64):
+                out, src = T.wk[o:o + 64, c0 + 32 * h:c0 + n:64], L[64 * h:64 * h + 64, l0:l0 + n // 64]
+                (s.activation(out, src, COPY) if q is s else v.tensor_copy(out, src)).then_inc(sem["ex" + x], 1)
 
-    v.memset(T.rcol[:], float(rank)).then_inc(sem["rc"], 1)
-    for a in range(4):
-        v.memset(T.tgb[32 * a:32 * a + 31, :], 0.0).then_inc(sem["tgz"], 1)
+    s.wait_ge(sem["wz"], 2)
+    s.wait_ge(sem["ida"], sum(len(bits(m)) for m in half))
+    expand(s, T.la, 0, "A")
+    for x in GROUPS:
+        copy_e(s, x, (0, 2) if x == "B2" else range(4))
+
+    for a in (0, 32):
+        v.memset(T.tgb[a:a + 29, :], 0.0).then_inc(sem["tgz"], 1)
     v.memset(T.mk[:], 1.0).then_inc(sem["mz"], 1)
-    v.memset(T.wk[:], 0.0).then_inc(sem["wz"], 1)
+    v.memset(T.wk[:, 0:3 * NC], 0.0).then_inc(sem["wz"], 1)
     v.wait_ge(sem["mz"], 1)
-    v.memset(T.mk[:, 0:256:32], 0.0).then_inc(sem["mz"], 1)
-    v.wait_ge(sem["tgz"], 4)
-    v.wait_ge(sem["ldtg"], 64)
+    v.memset(T.mk[:, 0:NC:32], 0.0).then_inc(sem["mz"], 1)
+    v.wait_ge(sem["tgz"], 2)
+    v.wait_ge(sem["ldtg"], 32)
     v.transpose(T.tt[:], T.tgb[:]).then_inc(sem["tt"], 1)
     v.wait_ge(sem["tt"], 1)
-    v.tensor_scalar(T.pv[:], T.tt[:, 159:256:32], 128.0, None, ADD).then_inc(sem["pvbm"], 1)
-    v.tensor_scalar(T.bm[:], T.tt[:, 287:384:32], 1.0 - EPS, None, SUB).then_inc(sem["pvbm"], 1)
-    v.wait_ge(sem["pvbm"], 2)
-    v.tensor_tensor(T.pb[:], T.pv[:], T.bm[:], MUL).then_inc(sem["pb"], 1)
-    v.wait_ge(sem["pb"], 1)
-    v.wait_ge(sem["eo"], 1)
-    v.tensor_tensor(T.keyl[0:64, 0:2], T.pb[0:64, 0:4:2], T.eo[0:64, 0:4:2], MUL).then_inc(sem["key"], 1)
-    v.tensor_tensor(T.keyl[64:128, 0:2], T.pb[64:128, 1:4:2], T.eo[64:128, 1:4:2], MUL).then_inc(sem["key"], 1)
-    v.wait_ge(sem["wz"], 1)
-    v.tensor_tensor(T.wk[:, 0:128:32], T.pb[:], T.eo[:, 0:4], MUL).then_inc(sem["exS"], 1)
-    v.wait_ge(sem["pi"], 1)
-    v.wait_ge(sem["ec"], 1)
-    for b in range(4):
-        v.tensor_scalar(T.kc[:, b:b + 1], T.pi[:, 0:1], BMUL[b], T.ec[:, 0:1], MUL, MUL).then_inc(sem["kc"], 1)
-
-    def expand(L, x):
-        c0, n = COL[x]
-        w2 = n // 64
-        for h in range(2):
-            for o in (0, 64):
-                v.tensor_copy(T.wk[o:o + 64, c0 + 32 * h:c0 + n:64], L[64 * h:64 * h + 64, 0:w2]).then_inc(sem["ex" + x], 1)
-        v.wait_ge(sem["ex" + x], 4)
+    v.tensor_scalar(T.ow[:], T.tt[:, 29:NC:32], 1024.0, None, MUL).then_inc(sem["ow"], 1)
+    for k in range(4):
+        v.tensor_scalar(T.pb[:, k:k + 1], T.tt[:, 32 * k + 31:32 * k + 32], 128.0, T.tt[:, 32 * k + 30:32 * k + 31],
+                        MUL, ADD).then_inc(sem["pb%d" % k], 1)
+    v.wait_ge(sem["r6"], 1)
+    v.wait_ge(sem["ow"], 1)
+    for k in range(4):
+        o, h = 64 * (k % 2), k // 2
+        v.wait_ge(sem["pb%d" % k], 1)
+        v.tensor_scalar(T.kk[o:o + 64, h:2 * len(C):2], T.r6[:, 0:len(C)], T.ow[:, k:k + 1], T.pb[:, k:k + 1],
+                        SUB, ADD).then_inc(sem["key"], 1)
+    v.memset(T.wk[:, 3 * NC:6 * NC], 0.0).then_inc(sem["wz"], 1)
 
     def scan(x):
         c0, n = COL[x]
-        v.tensor_tensor_scan(T.xs[:, c0:c0 + n], T.mk[:, 0:n], T.wk[:, c0:c0 + n], 0.0, MUL, ADD).then_inc(sem["sc" + x], 1)
+        v.tensor_tensor_scan(T.xs[:, c0:c0 + n], T.mk[:], T.wk[:, c0:c0 + n], 0.0, MUL, ADD).then_inc(sem["sc" + x], 1)
 
     def turn(x):
         c0, n = COL[x]
@@ -217,92 +214,92 @@ def rank_program(g, core, T, topo):
         v.quantize_mx(T.qe[:, c0:c0 + n], T.se[:, c0:c0 + n], T.e[:, 4 * c0:4 * (c0 + n)]).then_inc(sem["qe" + x], 1)
 
     v.wait_ge(sem["mz"], 2)
-    v.wait_ge(sem["exS"], 1)
+    v.wait_ge(sem["wz"], 2)
+    v.wait_ge(sem["key"], 4)
+    expand(v, T.kk, 2 * rank, "S")
+    v.wait_ge(sem["exS"], 4)
     scan("S"); turn("S")
-    v.wait_ge(sem["kc"], 4)
+    v.wait_ge(sem["kc"], 1)
     compare("S"); quant_o("S")
     for i in range(2):
         v.wait_ge(sem["ldt%d" % i], 16)
-        v.quantize_mx(T.qt[:, 256 * i:256 * i + 256], T.st[:, 256 * i:256 * i + 256], T.tabb[:, 1024 * i:1024 * i + 1024]).then_inc(sem["qt"], 1)
-    v.wait_ge(sem["ida"], len(near) * len(bits(topo.mask(core, C[near[0]]))))
-    expand(T.la, "A")
-    scan("A"); turn("A"); compare("A"); quant_o("A")
+        v.quantize_mx(T.qt[:, 256 * i:256 * i + 256], T.st[:, 256 * i:256 * i + 256],
+                      T.tabb[:, 1024 * i:1024 * i + 1024]).then_inc(sem["qt"], 1)
+    v.wait_ge(sem["exA"], 4)
+    scan("A0"); scan("A1"); turn("A0"); turn("A1")
+    compare("A0"); quant_o("A0")
+    compare("A1"); quant_o("A1")
     v.wait_ge(sem["ldw"], 16)
     v.quantize_mx(T.qw[:], T.sw[:], T.wb[:]).then_inc(sem["qw"], 1)
     quant_e("S")
-    for f in (1, 3): copy_e(v, "A", f)
-    quant_e("A")
-    v.wait_ge(sem["idb"], sum(len(bits(topo.mask(relay[j, rank], core))) for j in mine))
-    expand(T.lb, "B")
-    scan("B0"); scan("B1"); turn("B0"); scan("B2"); turn("B1")
-    compare("B0"); turn("B2"); quant_o("B0")
-    compare("B1"); quant_o("B1")
+    quant_e("A0")
+    v.wait_ge(sem["idb"], n_relay * len(mine))
+    expand(v, T.lb, 0, "B")
+    v.wait_ge(sem["exB"], 4)
+    scan("B0"); scan("B1"); turn("B0"); scan("B2")
+    compare("B0"); turn("B1"); quant_o("B0")
+    quant_e("A1")
+    compare("B1"); turn("B2"); quant_o("B1")
     compare("B2"); quant_o("B2")
     quant_e("B0")
     quant_e("B1")
-    for f in (1, 3): copy_e(v, "B2", f)
+    copy_e(v, "B2", (1, 3))
     quant_e("B2")
     v.wait_ge(sem["yz"], 1)
-    v.tensor_copy(T.yb[:], T.z[:, 2048:2048 + NC]).then_inc(sem["yc"], 1)
+    v.tensor_copy(T.yb[:], T.z[:, 0:NC]).then_inc(sem["yc"], 1)
 
     t.wait_ge(sem["qt"], 2)
-    free = {"S": None, "A": None, "B0": "S", "B1": "A", "B2": "B0"}
-    for x in GROUPS:
+    for i, x in enumerate(GROUPS):
         c0, n = COL[x]
         t.wait_ge(sem["qo" + x], 1)
-        if free[x]:
-            t.wait_ge(sem["ce" + free[x]], 4)
+        if i > 1:
+            t.wait_ge(sem["ce" + GROUPS[i - 2]], 4)
         for f in range(4):
             b0 = 512 * (BANK[x] + f)
             t.matmul_mx(T.z[:, b0:b0 + n], T.qt[:, 128 * f:128 * f + 128], T.st[:, 128 * f:128 * f + 128],
                         T.qo[:, c0:c0 + n], T.so[:, c0:c0 + n], True, True).then_inc(sem["z%s%d" % (x, f)], 1)
-    yo = T.z[:, 2048:2048 + NC]
+    yo = T.z[:, 0:NC]
     t.wait_ge(sem["ceB1"], 4)
     t.wait_ge(sem["qw"], 1)
     t.wait_ge(sem["qeS"], 1)
     t.matmul_mx(yo, T.qw[:], T.sw[:], T.qe[:, 0:NC], T.se[:, 0:NC], True, False)
-    half = len(bits(topo.mask(core, C[near[0]]))) // len(near)
-    for i in range(len(near)):
-        t.wait_ge(sem["ea%d" % i], 2 * half)
-        t.matmul_mx(yo, T.qw[:], T.sw[:], T.le[:, NC * i:NC * i + NC], T.ls[:, NC * i:NC * i + NC], False, False)
-    arr = sorted(range(len(mine)), key=lambda i: order[mine[i]].index(rank))
-    for i in arr:
-        p = 2 + i
-        t.wait_ge(sem["eb%d" % i], 2 * len(bits(topo.mask(relay[mine[i], rank], core))))
-        m = t.matmul_mx(yo, T.qw[:], T.sw[:], T.le[:, NC * p:NC * p + NC], T.ls[:, NC * p:NC * p + NC], False, i == arr[-1])
+    arr = [("A%d" % direct[j].index(rank), i, "ea%d" % i, 2 * len(bits(off))) for i, j in enumerate(near)]
+    arr += [("B%d" % order[j].index(rank), len(near) + i, "eb%d" % i, 2 * n_relay) for i, j in enumerate(mine)]
+    arr.sort(key=lambda a: GROUPS.index(a[0]))
+    for x, p, rsem, n in arr:
+        t.wait_ge(sem[rsem], n)
+        m = t.matmul_mx(yo, T.qw[:], T.sw[:], T.le[:, NC * p:NC * p + NC], T.ls[:, NC * p:NC * p + NC], False, p == arr[-1][1])
     m.then_inc(sem["yz"], 1)
 
-    g.iota(T.pi[:, 0:1], [[0, 1]], 128, 1, allow_small_or_imprecise_dtypes=True).then_inc(sem["pi"], 1)
-    rel = [relay[rank, j] for j in mine]
-    on = topo.mask(core, rel[0])
-    off = topo.mask(core, C[near[0]])
+    g.iota(T.r6[:], [[1024, 8]], -256, 0, allow_small_or_imprecise_dtypes=True).then_inc(sem["r6"], 1)
+    g.iota(T.kc[:, 0:4], [[128, 4]], -256, 1, allow_small_or_imprecise_dtypes=True).then_inc(sem["kc"], 1)
     sent = [0]
 
-    def move(dsts, mask, rsem, src, outs):
-        return RemoteDMATransfer(dst_ids=[DstId(rid=topo.addr(d)[0], pnc=topo.addr(d)[1]) for d in dsts],
-                                 dma_engine_mask=mask, remote_sem=sem[rsem], srcs=[src], dsts=outs)
+    def move(d, mask, rsem, src, out):
+        return RemoteDMATransfer(dst_ids=[DstId(rid=topo.addr(d)[0], pnc=topo.addr(d)[1])],
+                                 dma_engine_mask=mask, remote_sem=sem[rsem], srcs=[src], dsts=[out])
 
     def send(transfers, masks):
         g.remote_dma_fused(transfers, local_sem=sem["loc"])
         sent[0] += sum(len(bits(m)) for m in masks)
 
-    g.wait_ge(sem["key"], 2)
-    send([move(rel, on & ~off, "rid", T.keyl[:, 0:2], [T.rk[:, 0:2]] * len(rel))], [on & ~off])
+    g.wait_ge(sem["key"], 4)
+    send([move(d, m, "rid", T.kk[:, 2 * j:2 * j + 2], T.rk[:, 0:2]) for d, j, m in zip(rel, mine, idm)], idm)
     ai = [direct[j].index(rank) for j in near]
-    send([move([C[j] for j in near], off, "ida", T.keyl[:, 0:2], [T.la[:, 2 * a:2 * a + 2] for a in ai])], [off])
-    g.wait_ge(sem["qeA"], 1)
-    ms = split(off, len(near))
-    jobs = list(enumerate(zip(near, ai, ms)))
-    send([move([C[j]], m, "ea%d" % a, T.qe[:, 128 + NC * k:256 + NC * k].bitcast(dt.uint8),
-               [T.le[:, NC * a:NC * a + NC].bitcast(dt.uint8)]) for k, (j, a, m) in jobs], ms)
-    send([move([C[j]], m, "ea%d" % a, T.se[:, 128 + NC * k:256 + NC * k], [T.ls[:, NC * a:NC * a + NC]])
-          for k, (j, a, m) in jobs], ms)
+    send([move(C[j], m, "ida", T.kk[:, 2 * j:2 * j + 2], T.la[:, 2 * a:2 * a + 2]) for j, a, m in zip(near, ai, half)], half)
+    for k, (j, a) in enumerate(zip(near, ai)):
+        c0 = COL["A%d" % k][0]
+        g.wait_ge(sem["qeA%d" % k], 1)
+        send([move(C[j], off, "ea%d" % a, T.qe[:, c0:c0 + NC].bitcast(dt.uint8), T.le[:, NC * a:NC * a + NC].bitcast(dt.uint8))], [off])
+        send([move(C[j], off, "ea%d" % a, T.se[:, c0:c0 + NC], T.ls[:, NC * a:NC * a + NC])], [off])
 
     def codes(k):
-        send([move([rel[k]], on, "rcod", T.qe[:, 384 + NC * k:512 + NC * k].bitcast(dt.uint8), [T.rc[:, 0:NC].bitcast(dt.uint8)])], [on])
+        c0 = COL["B%d" % k][0]
+        send([move(rel[k], on, "rcod", T.qe[:, c0:c0 + NC].bitcast(dt.uint8), T.rc[:, 0:NC].bitcast(dt.uint8))], [on])
 
     def scales(k, by, rsem, col):
-        send([move([rel[by]], on, rsem, T.se[:, 384 + NC * k:512 + NC * k], [T.rs[:, col:col + NC]])], [on])
+        c0 = COL["B%d" % k][0]
+        send([move(rel[by], on, rsem, T.se[:, c0:c0 + NC], T.rs[:, col:col + NC])], [on])
 
     for k in (0, 1):
         g.wait_ge(sem["qeB%d" % k], 1)

from concourse.bass import DstId, RemoteDMATransfer
from concourse.mybir import dt, AluOpType, ActivationFunctionType

NC = 128

SCRATCH = {
    "r6": ("sbuf", [64, 8], "float32"),
    "kc": ("sbuf", [128, 8], "bfloat16"),
    "tgb": ("sbuf", [64, 128], "bfloat16"),
    "tt": ("sbuf", [64, 128], "bfloat16"),
    "ow": ("sbuf", [64, 4], "float32"),
    "pb": ("sbuf", [64, 4], "float32"),
    "kk": ("sbuf", [128, 16], "bfloat16"),
    "la": ("sbuf", [128, 8], "bfloat16"),
    "lb": ("sbuf", [128, 8], "bfloat16"),
    "wk": ("sbuf", [128, 768], "bfloat16"),
    "mk": ("sbuf", [128, 128], "bfloat16"),
    "xs": ("sbuf", [128, 768], "bfloat16"),
    "xt": ("sbuf", [128, 768], "bfloat16"),
    "o": ("sbuf", [128, 3072], "bfloat16"),
    "qo": ("sbuf", [128, 768], "float8_e4m3fn_x4"),
    "so": ("sbuf", [128, 768], "uint8"),
    "e": ("sbuf", [128, 3072], "bfloat16"),
    "qe": ("sbuf", [128, 768], "float8_e4m3fn_x4"),
    "se": ("sbuf", [128, 768], "uint8"),
    "tabb": ("sbuf", [128, 2048], "bfloat16"),
    "qt": ("sbuf", [128, 512], "float8_e4m3fn_x4"),
    "st": ("sbuf", [128, 512], "uint8"),
    "wb": ("sbuf", [128, 512], "bfloat16"),
    "qw": ("sbuf", [128, 128], "float8_e4m3fn_x4"),
    "sw": ("sbuf", [128, 128], "uint8"),
    "le": ("sbuf", [128, 640], "float8_e4m3fn_x4"),
    "ls": ("sbuf", [128, 640], "uint8"),
    "rk": ("sbuf", [128, 8], "bfloat16"),
    "rc": ("sbuf", [128, 128], "float8_e4m3fn_x4"),
    "rs": ("sbuf", [128, 256], "uint8"),
    "yb": ("sbuf", [128, 128], "float32"),
    "z": ("psum", [128, 4096], "float32"),
}
GROUPS = ("S", "A0", "A1", "B0", "B1", "B2")
SEMAPHORES = (
    ["ldtg", "ldt0", "ldt1", "ldw", "sty", "r6", "kc", "tgz", "wz", "mz", "tt", "ow", "pb0", "pb1", "pb2", "pb3", "key",
     "qt", "qw", "yz", "yc", "loc", "ida", "idb", "ea0", "ea1", "eb0", "eb1", "eb2", "rid", "rcod", "rsca", "rscb", "rloc",
     "exS", "exA", "exB"]
    + ["%s%s" % (n, x) for n in ("sc", "xt", "oh", "qo", "ce", "qe") for x in GROUPS]
    + ["z%s%d" % (x, f) for x in GROUPS for f in range(4)]
)


def bits(mask):
    return [1 << i for i in range(mask.bit_length()) if mask >> i & 1]


def split(mask, n):
    b = bits(mask)
    k = len(b) // n
    return [sum(b[i * k:(i + 1) * k]) for i in range(n)]


def id_masks(on, off, n):
    return sorted(split(on, 4), key=lambda m: m & off)[:n]


def make_plan(T, topo):
    C = list(T.cores)
    R = range(len(C))
    direct = {r: [j for j in R if j != r and topo.may_write(C[r], C[j])] for r in R}
    cross = {r: [j for j in R if j != r and not topo.may_write(C[r], C[j])] for r in R}
    lane, relay, order = {}, {}, {}
    for r in R:
        cand = [c for c in range(topo.CHIPS * topo.CORES_PER_CHIP)
                if topo.chip(c) == topo.chip(C[r]) and c not in C and all(topo.may_write(c, C[j]) for j in cross[r])]
        cand.sort(key=lambda c: (topo.die(c) != topo.die(C[r]), c))
        for d, j in enumerate(cross[r]):
            lane[r, j] = (cross[j].index(r) + d) % len(cross[r])
            relay[r, j] = cand[lane[r, j]]
        order[r] = sorted(cross[r], key=lambda j: (lane[r, j] + 1) % len(cross[r]))
    return C, direct, cross, relay, order


def run_relay(g, core, T, topo, C, order, r, j):
    sem = T.sem
    off = topo.mask(core, C[j])
    on = topo.mask(C[r], core)
    n_on = len(bits(on))
    n_id = len(bits(id_masks(on, off, len(order[r]))[0]))
    k = order[r].index(j)
    sent = [0]

    def scales(to, col):
        rid, pid = topo.addr(C[to])[:2]
        i = order[to].index(r)
        g.remote_dma(T.ls[:, NC * (2 + i):NC * (3 + i)], T.rs[:, col:col + NC], sem["eb%d" % i], sem["rloc"], pid, rid, off)
        sent[0] += len(bits(off))

    rid, pid = topo.addr(C[j])[:2]
    i = order[j].index(r)
    g.wait_ge(sem["rid"], n_id)
    g.remote_dma(T.lb[:, 2 * i:2 * i + 2], T.rk[:, 0:2], sem["idb"], sem["rloc"], pid, rid, off)
    if k < 2:
        g.wait_ge(sem["rsca"], n_on)
        scales(j, 0)
    g.wait_ge(sem["rcod"], n_on)
    g.remote_dma(T.le[:, NC * (2 + i):NC * (3 + i)].bitcast(dt.uint8), T.rc[:, 0:NC].bitcast(dt.uint8),
                 sem["eb%d" % i], sem["rloc"], pid, rid, off)
    if k == 0:
        g.wait_ge(sem["rscb"], n_on)
        scales(order[r][2], NC)
    g.wait_ge(sem["rloc"], sent[0] + 2 * len(bits(off)))


def rank_program(g, core, T, topo):
    C, direct, cross, relay, order = make_plan(T, topo)
    rank = T.rank_of(core)
    if rank is None:
        for (r, j), c in relay.items():
            if c == core:
                run_relay(g, core, T, topo, C, order, r, j)
        return
    sem = T.sem
    v, s, t, sy = g.vector, g.scalar, g.tensor, g.sync
    ADD, SUB, MUL, EQ = AluOpType.add, AluOpType.subtract, AluOpType.mult, AluOpType.is_equal
    COPY = ActivationFunctionType.Copy
    mine, near = order[rank], direct[rank]
    COL = {x: (NC * i, NC) for i, x in enumerate(GROUPS)}
    COL["A"], COL["B"] = (NC, 2 * NC), (3 * NC, 3 * NC)
    BANK = {x: 4 * (i % 2) for i, x in enumerate(GROUPS)}
    rel = [relay[rank, j] for j in mine]
    on = topo.mask(core, rel[0])
    off = topo.mask(core, C[near[0]])
    idm = id_masks(on, off, len(rel))
    half = split(off, len(near))
    n_relay = len(bits(topo.mask(rel[0], C[mine[0]])))

    sy.dma_start(T.tgb[29:32, :], T.tg[0:1, :]).then_inc(sem["ldtg"], 16)
    s.dma_start(T.tgb[61:64, :], T.tg[1:2, :]).then_inc(sem["ldtg"], 16)
    sy.dma_start(T.tabb[:, 0:1024], T.tab[:, 0:1024]).then_inc(sem["ldt0"], 16)
    sy.dma_start(T.tabb[:, 1024:2048], T.tab[:, 1024:2048]).then_inc(sem["ldt1"], 16)
    sy.dma_start(T.wb[:], T.w[:]).then_inc(sem["ldw"], 16)
    sy.wait_ge(sem["yc"], 1)
    sy.dma_start(T.y[:], T.yb[:]).then_inc(sem["sty"], 16)
    sy.wait_ge(sem["sty"], 16)

    def copy_e(q, x, fs):
        c0, n = COL[x]
        for f in fs:
            b0 = 512 * (BANK[x] + f)
            q.wait_ge(sem["z%s%d" % (x, f)], 1)
            out = T.e[:, 4 * c0 + f:4 * (c0 + n):4]
            if q is s:
                s.activation(out, T.z[:, b0:b0 + n], COPY).then_inc(sem["ce" + x], 1)
            else:
                v.tensor_copy(out, T.z[:, b0:b0 + n]).then_inc(sem["ce" + x], 1)

    def expand(q, L, l0, x):
        c0, n = COL[x]
        for h in (0, 1):
            for o in (0, 64):
                out, src = T.wk[o:o + 64, c0 + 32 * h:c0 + n:64], L[64 * h:64 * h + 64, l0:l0 + n // 64]
                (s.activation(out, src, COPY) if q is s else v.tensor_copy(out, src)).then_inc(sem["ex" + x], 1)

    s.wait_ge(sem["wz"], 2)
    s.wait_ge(sem["ida"], sum(len(bits(m)) for m in half))
    expand(s, T.la, 0, "A")
    for x in GROUPS:
        copy_e(s, x, (0, 2) if x == "B2" else range(4))

    for a in (0, 32):
        v.memset(T.tgb[a:a + 29, :], 0.0).then_inc(sem["tgz"], 1)
    v.memset(T.mk[:], 1.0).then_inc(sem["mz"], 1)
    v.memset(T.wk[:, 0:3 * NC], 0.0).then_inc(sem["wz"], 1)
    v.wait_ge(sem["mz"], 1)
    v.memset(T.mk[:, 0:NC:32], 0.0).then_inc(sem["mz"], 1)
    v.wait_ge(sem["tgz"], 2)
    v.wait_ge(sem["ldtg"], 32)
    v.transpose(T.tt[:], T.tgb[:]).then_inc(sem["tt"], 1)
    v.wait_ge(sem["tt"], 1)
    v.tensor_scalar(T.ow[:], T.tt[:, 29:NC:32], 1024.0, None, MUL).then_inc(sem["ow"], 1)
    for k in range(4):
        v.tensor_scalar(T.pb[:, k:k + 1], T.tt[:, 32 * k + 31:32 * k + 32], 128.0, T.tt[:, 32 * k + 30:32 * k + 31],
                        MUL, ADD).then_inc(sem["pb%d" % k], 1)
    v.wait_ge(sem["r6"], 1)
    v.wait_ge(sem["ow"], 1)
    for k in range(4):
        o, h = 64 * (k % 2), k // 2
        v.wait_ge(sem["pb%d" % k], 1)
        v.tensor_scalar(T.kk[o:o + 64, h:2 * len(C):2], T.r6[:, 0:len(C)], T.ow[:, k:k + 1], T.pb[:, k:k + 1],
                        SUB, ADD).then_inc(sem["key"], 1)
    v.memset(T.wk[:, 3 * NC:6 * NC], 0.0).then_inc(sem["wz"], 1)

    def scan(x):
        c0, n = COL[x]
        v.tensor_tensor_scan(T.xs[:, c0:c0 + n], T.mk[:], T.wk[:, c0:c0 + n], 0.0, MUL, ADD).then_inc(sem["sc" + x], 1)

    def turn(x):
        c0, n = COL[x]
        v.wait_ge(sem["sc" + x], 1)
        v.transpose(T.xt[:, c0:c0 + n], T.xs[:, c0:c0 + n]).then_inc(sem["xt" + x], 1)

    def compare(x):
        c0, n = COL[x]
        v.wait_ge(sem["xt" + x], 1)
        for b in range(4):
            v.tensor_scalar(T.o[:, 4 * c0 + b:4 * (c0 + n):4], T.xt[:, c0:c0 + n], T.kc[:, b:b + 1], None, EQ).then_inc(sem["oh" + x], 1)

    def quant_o(x):
        c0, n = COL[x]
        v.wait_ge(sem["oh" + x], 4)
        v.quantize_mx(T.qo[:, c0:c0 + n], T.so[:, c0:c0 + n], T.o[:, 4 * c0:4 * (c0 + n)]).then_inc(sem["qo" + x], 1)

    def quant_e(x):
        c0, n = COL[x]
        v.wait_ge(sem["ce" + x], 4)
        v.quantize_mx(T.qe[:, c0:c0 + n], T.se[:, c0:c0 + n], T.e[:, 4 * c0:4 * (c0 + n)]).then_inc(sem["qe" + x], 1)

    v.wait_ge(sem["mz"], 2)
    v.wait_ge(sem["wz"], 2)
    v.wait_ge(sem["key"], 4)
    expand(v, T.kk, 2 * rank, "S")
    v.wait_ge(sem["exS"], 4)
    scan("S"); turn("S")
    v.wait_ge(sem["kc"], 1)
    compare("S"); quant_o("S")
    for i in range(2):
        v.wait_ge(sem["ldt%d" % i], 16)
        v.quantize_mx(T.qt[:, 256 * i:256 * i + 256], T.st[:, 256 * i:256 * i + 256],
                      T.tabb[:, 1024 * i:1024 * i + 1024]).then_inc(sem["qt"], 1)
    v.wait_ge(sem["exA"], 4)
    scan("A0"); scan("A1"); turn("A0"); turn("A1")
    compare("A0"); quant_o("A0")
    compare("A1"); quant_o("A1")
    v.wait_ge(sem["ldw"], 16)
    v.quantize_mx(T.qw[:], T.sw[:], T.wb[:]).then_inc(sem["qw"], 1)
    quant_e("S")
    quant_e("A0")
    v.wait_ge(sem["idb"], n_relay * len(mine))
    expand(v, T.lb, 0, "B")
    v.wait_ge(sem["exB"], 4)
    scan("B0"); scan("B1"); turn("B0"); scan("B2")
    compare("B0"); turn("B1"); quant_o("B0")
    quant_e("A1")
    compare("B1"); turn("B2"); quant_o("B1")
    compare("B2"); quant_o("B2")
    quant_e("B0")
    quant_e("B1")
    copy_e(v, "B2", (1, 3))
    quant_e("B2")
    v.wait_ge(sem["yz"], 1)
    v.tensor_copy(T.yb[:], T.z[:, 0:NC]).then_inc(sem["yc"], 1)

    t.wait_ge(sem["qt"], 2)
    for i, x in enumerate(GROUPS):
        c0, n = COL[x]
        t.wait_ge(sem["qo" + x], 1)
        if i > 1:
            t.wait_ge(sem["ce" + GROUPS[i - 2]], 4)
        for f in range(4):
            b0 = 512 * (BANK[x] + f)
            t.matmul_mx(T.z[:, b0:b0 + n], T.qt[:, 128 * f:128 * f + 128], T.st[:, 128 * f:128 * f + 128],
                        T.qo[:, c0:c0 + n], T.so[:, c0:c0 + n], True, True).then_inc(sem["z%s%d" % (x, f)], 1)
    yo = T.z[:, 0:NC]
    t.wait_ge(sem["ceB1"], 4)
    t.wait_ge(sem["qw"], 1)
    t.wait_ge(sem["qeS"], 1)
    t.matmul_mx(yo, T.qw[:], T.sw[:], T.qe[:, 0:NC], T.se[:, 0:NC], True, False)
    arr = [("A%d" % direct[j].index(rank), i, "ea%d" % i, 2 * len(bits(off))) for i, j in enumerate(near)]
    arr += [("B%d" % order[j].index(rank), len(near) + i, "eb%d" % i, 2 * n_relay) for i, j in enumerate(mine)]
    arr.sort(key=lambda a: GROUPS.index(a[0]))
    for x, p, rsem, n in arr:
        t.wait_ge(sem[rsem], n)
        m = t.matmul_mx(yo, T.qw[:], T.sw[:], T.le[:, NC * p:NC * p + NC], T.ls[:, NC * p:NC * p + NC], False, p == arr[-1][1])
    m.then_inc(sem["yz"], 1)

    g.iota(T.r6[:], [[1024, 8]], -256, 0, allow_small_or_imprecise_dtypes=True).then_inc(sem["r6"], 1)
    g.iota(T.kc[:, 0:4], [[128, 4]], -256, 1, allow_small_or_imprecise_dtypes=True).then_inc(sem["kc"], 1)
    sent = [0]

    def move(d, mask, rsem, src, out):
        return RemoteDMATransfer(dst_ids=[DstId(rid=topo.addr(d)[0], pnc=topo.addr(d)[1])],
                                 dma_engine_mask=mask, remote_sem=sem[rsem], srcs=[src], dsts=[out])

    def send(transfers, masks):
        g.remote_dma_fused(transfers, local_sem=sem["loc"])
        sent[0] += sum(len(bits(m)) for m in masks)

    g.wait_ge(sem["key"], 4)
    send([move(d, m, "rid", T.kk[:, 2 * j:2 * j + 2], T.rk[:, 0:2]) for d, j, m in zip(rel, mine, idm)], idm)
    ai = [direct[j].index(rank) for j in near]
    send([move(C[j], m, "ida", T.kk[:, 2 * j:2 * j + 2], T.la[:, 2 * a:2 * a + 2]) for j, a, m in zip(near, ai, half)], half)
    for k, (j, a) in enumerate(zip(near, ai)):
        c0 = COL["A%d" % k][0]
        g.wait_ge(sem["qeA%d" % k], 1)
        send([move(C[j], off, "ea%d" % a, T.qe[:, c0:c0 + NC].bitcast(dt.uint8), T.le[:, NC * a:NC * a + NC].bitcast(dt.uint8))], [off])
        send([move(C[j], off, "ea%d" % a, T.se[:, c0:c0 + NC], T.ls[:, NC * a:NC * a + NC])], [off])

    def codes(k):
        c0 = COL["B%d" % k][0]
        send([move(rel[k], on, "rcod", T.qe[:, c0:c0 + NC].bitcast(dt.uint8), T.rc[:, 0:NC].bitcast(dt.uint8))], [on])

    def scales(k, by, rsem, col):
        c0 = COL["B%d" % k][0]
        send([move(rel[by], on, rsem, T.se[:, c0:c0 + NC], T.rs[:, col:col + NC])], [on])

    for k in (0, 1):
        g.wait_ge(sem["qeB%d" % k], 1)
        scales(k, k, "rsca", 0)
        codes(k)
    g.wait_ge(sem["qeB2"], 1)
    codes(2)
    scales(2, 0, "rscb", NC)
    g.wait_ge(sem["loc"], sent[0])
